import numpy as np
import ml_dtypes


def mxq(x, axis, fmt="e4m3"):
    dtype, down = {"e4m3": (ml_dtypes.float8_e4m3fn, 7), "e5m2": (ml_dtypes.float8_e5m2, 14)}[fmt]
    v = np.moveaxis(np.asarray(x, np.float32).astype(ml_dtypes.bfloat16).astype(np.float64), axis, -1)
    blocks = v.reshape(v.shape[:-1] + (-1, 32))
    amax = np.abs(blocks).max(-1, keepdims=True)
    byte = np.maximum(np.where(amax > 0, np.frexp(amax)[1] - 1 + 127, 0) - down, 1)
    scale = np.exp2(byte - 127.0)
    codes = (blocks / scale).astype(np.float32).astype(dtype).astype(np.float64)
    return np.moveaxis((codes * scale).reshape(v.shape), -1, axis)


WIDE = False


def mx_kscale(k):
    if not WIDE:
        return np.ones(k)
    levels = np.array([10, -10, 5, -5, 0])
    if k % 512:
        return np.exp2(np.random.permutation(np.resize(levels, k // 32))).repeat(32)
    a = np.empty((k // 512, 16))
    for p in range(k // 512):
        a[p, :8] = np.random.permutation(np.resize(levels, 8))
        for g in range(8):
            far = levels[np.abs(levels - a[p, g]) >= 10]
            a[p, g + 8] = far[np.random.randint(len(far))]
    return np.exp2(a.ravel()).repeat(32)


def f64(x):
    return np.asarray(x).astype(np.float64)


def striped(idx):
    return np.tile(idx.reshape(-1, 16).T, (8, 1)).astype(np.uint16)


def unstriped(offs):
    return offs[:16].T.reshape(-1).astype(np.int64)


E2M1 = np.array([0.0, 0.5, 1.0, 1.5, 2.0, 3.0, 4.0, 6.0, -0.0, -0.5, -1.0, -1.5, -2.0, -3.0, -4.0, -6.0])


def pack_weight(w, fmt):
    k, n = w.shape
    w = f64(np.asarray(w, np.float32).astype(ml_dtypes.bfloat16)).reshape(k // 32, 32, n)
    amax = np.abs(w).max(1)
    if fmt == "e4m3":
        byte = np.frexp(amax)[1] - 1 + 127 - 7
    else:
        mant, ex = np.frexp(amax / 6.0)
        byte = np.where(mant > 0.5, ex, ex - 1) + 127
    byte = np.clip(np.where(amax > 0, byte, 1), 1, 254)
    scaled = (w * np.exp2(127.0 - byte)[:, None, :]).reshape(k, n).astype(np.float32)
    by_word = np.ascontiguousarray(scaled.reshape(k // 512, 128, 4, n).transpose(0, 1, 3, 2))
    if fmt == "e4m3":
        words = by_word.astype(ml_dtypes.float8_e4m3fn).view(np.uint8)
    else:
        c = by_word.astype(ml_dtypes.float4_e2m1fn).view(np.uint8) & 0xF
        words = (c[..., 0::2] | (c[..., 1::2] << 4)).reshape(k // 512, 128, 2 * n)
    return np.ascontiguousarray(words), np.ascontiguousarray(byte.astype(np.uint8).reshape(k // 512, 16, n))


def unpack_weight(words, scales, fmt):
    g, _, n = scales.shape
    words = np.ascontiguousarray(words).reshape(g, 128, n, -1)
    if fmt == "e4m3":
        vals = words.view(ml_dtypes.float8_e4m3fn).astype(np.float64)
    else:
        nib = np.empty((g, 128, n, 4), np.uint8)
        nib[..., 0::2] = words & 0xF
        nib[..., 1::2] = words >> 4
        vals = E2M1[nib]
    vals = vals * np.repeat(np.exp2(scales.astype(np.float64) - 127.0), 8, axis=1)[..., None]
    return vals.transpose(0, 1, 3, 2).reshape(g * 512, n)


def gelu(v):
    return 0.5 * v * (1.0 + np.tanh(np.sqrt(2.0 / np.pi) * (v + 0.044715 * v**3)))


K, K2, H, N, T, T2, S = 1024, 512, 1024, 512, 2048, 2048, 1024

def setup_inputs():
    n = np.random.standard_normal
    s, s2 = mx_kscale(K)[:, None], mx_kscale(K2)[:, None]
    u = mx_kscale(H)[:, None]
    tab_words, tab_scales = pack_weight(n((K, T)) * s, "e4m3")
    tab2_words, tab2_scales = pack_weight(n((K2, T2)) * s2, "e4m3")
    wy_words, wy_scales = pack_weight(0.8 * n((K2, H)) / np.sqrt(K2) / s2, "e2m1")
    return {
        "tab_words": tab_words, "tab_scales": tab_scales,
        "offs": striped(np.random.permutation(T)[:S]),
        "tab2_words": tab2_words, "tab2_scales": tab2_scales,
        "offs2": striped(np.random.permutation(T2)[:S]),
        "wu": (0.8 * n((K, H)) / np.sqrt(K) / s).astype(np.float32),
        "wy_words": wy_words, "wy_scales": wy_scales,
        "bx": (0.5 * n(H)).astype(np.float32),
        "gain": (np.exp(0.3 * n(H)) * u[:, 0]).astype(np.float32),
        "wp": (n((H, N)) / np.sqrt(H) / u).astype(np.float32),
        "sp": (0.5 * n(N)).astype(np.float32),
    }

def reference(tab_words, tab_scales, offs, tab2_words, tab2_scales, offs2,
              wu, wy_words, wy_scales, bx, gain, wp, sp):
    v = unpack_weight(tab_words, tab_scales, "e4m3")[:, unstriped(offs)]
    v2 = unpack_weight(tab2_words, tab2_scales, "e4m3")[:, unstriped(offs2)]
    wuq = mxq(f64(wu), 0, "e4m3")
    wy = unpack_weight(wy_words, wy_scales, "e2m1")
    z = wuq.T @ v + wy.T @ v2
    x = f64(gain)[:, None] * np.tanh(z + f64(bx)[:, None])
    xq = mxq(x, 0, "e4m3")
    wpq = mxq(f64(wp), 0, "e4m3")
    y = wpq.T @ xq
    return y - f64(sp)[:, None]

@@ -1,0 +1,287 @@
+from contextlib import ExitStack
+
+import concourse.mybir as mybir
+from concourse.masks import make_identity
+
+K, K2, H, N, T, S = 1024, 512, 1024, 512, 2048, 1024
+FLOPS = 2 * S * (K * H + K2 * H + H * N)
+
+F32 = mybir.dt.float32
+BF16 = mybir.dt.bfloat16
+I32 = mybir.dt.int32
+U32 = mybir.dt.uint32
+U16 = mybir.dt.uint16
+U8 = mybir.dt.uint8
+FP8X4 = mybir.dt.float8_e4m3fn_x4
+FP4X4 = mybir.dt.float4_e2m1fn_x4
+ACT = mybir.ActivationFunctionType
+ALU = mybir.AluOpType
+
+P = 128
+PASS = 512
+CHUNK = 512
+AL = 64
+
+
+def tile_list_predictive_control_error_kernel(
+    tc, tab_words, tab_scales, offs, tab2_words, tab2_scales, offs2,
+    wu, wy_words, wy_scales, bx, gain, wp, sp, out,
+):
+    nc = tc.nc
+    with ExitStack() as ctx:
+        keep = ctx.enter_context(tc.tile_pool(name="keep", bufs=1))
+        psum_vec = ctx.enter_context(tc.psum_pool(name="psum_vec", bufs=1))
+        psum = ctx.enter_context(tc.psum_pool(name="psum", bufs=7))
+
+        def held(name, shape, dtype):
+            return keep.tile(shape, dtype, name=name, align_bytes=AL)
+
+        list1 = held("list1", [P, S // 16], U16)
+        list2 = held("list2", [P, S // 16], U16)
+        tab_w = [held("tab_w%d" % a, [P, T], I32) for a in range(2)]
+        tab2_w = held("tab2_w", [P, T], I32)
+        tab_s = held("tab_s", [P, T // 4], I32)
+        tab2_s = held("tab2_s", [P, T // 4], I32)
+        wy_w_raw = held("wy_w_raw", [P, H // 2], I32)
+        wy_s_raw = held("wy_s_raw", [P, H // 4], I32)
+        wy_w = held("wy_w", [P, H // 2], I32)
+        wy_s = held("wy_s", [P, H // 4], I32)
+        v_w = [held("v_w%d" % a, [P, S], U32) for a in range(2)]
+        v_s = held("v_s", [P, S], U8)
+        v2_w = held("v2_w", [P, S], U32)
+        v2_s = held("v2_s", [P, S], U8)
+        wu_raw = {(a, b): held("wu_raw%d%d" % (a, b), [P, 4, PASS], F32) for a in range(2) for b in range(2)}
+        wu_bf = {(a, b): held("wu_bf%d%d" % (a, b), [P, PASS, 4], BF16) for a in range(2) for b in range(2)}
+        wu_w = {(a, b): held("wu_w%d%d" % (a, b), [P, PASS], U32) for a in range(2) for b in range(2)}
+        wu_s = {(a, b): held("wu_s%d%d" % (a, b), [P, PASS], U8) for a in range(2) for b in range(2)}
+        wp_raw = [held("wp_raw%d" % b, [P, 4, N], F32) for b in range(2)]
+        wp_bf = [held("wp_bf%d" % b, [P, N, 4], BF16) for b in range(2)]
+        wp_w = [held("wp_w%d" % b, [P, N], U32) for b in range(2)]
+        wp_s = [held("wp_s%d" % b, [P, N], U8) for b in range(2)]
+        x_w = [held("x_w%d" % b, [P, S], U32) for b in range(2)]
+        x_s = [held("x_s%d" % b, [P, S], U8) for b in range(2)]
+        th = {(b, c): held("th%d%d" % (b, c), [P, 4, CHUNK], F32) for b in range(2) for c in range(2)}
+        xb = {(b, c): held("xb%d%d" % (b, c), [P, CHUNK, 4], BF16) for b in range(2) for c in range(2)}
+        res = held("res", [P, 4, S], F32)
+        vec_rows = held("vec_rows", [P, 2, P], F32)
+        ident = held("ident", [P, P], F32)
+        bias = held("bias", [P, 2, 4], F32)
+        neg_sp = held("neg_sp", [P, 4], F32)
+        vec_ps = psum_vec.tile([P, 2, P], F32, name="vec_ps")
+
+        nc.gpsimd.memset(tab_s[:], 0)
+        nc.vector.memset(tab2_s[:], 0)
+        nc.gpsimd.memset(vec_rows[:], 0.0)
+        nc.gpsimd.memset(wy_s_raw[:], 0)
+
+        def load_words(dst, words, a):
+            nc.sync.dma_start(out=dst[:], in_=words[a].rearrange("p t i -> p (t i)").bitcast(I32))
+
+        def load_wu(a, b):
+            rows = wu[a * PASS:(a + 1) * PASS, b * PASS:(b + 1) * PASS]
+            nc.sync.dma_start(out=wu_raw[a, b][:], in_=rows.rearrange("(p j) c -> p j c", j=4))
+
+        def load_wp(b):
+            rows = wp[b * PASS:(b + 1) * PASS, :].rearrange("(g t q) n -> t g q n", t=4, q=8)
+            for t in range(4):
+                nc.sync.dma_start(out=wp_raw[b][:, t, :], in_=rows[t])
+
+        def load_scales(queue, dst, scales):
+            passes = scales.shape[0]
+            rows = scales.bitcast(I32)
+            for quad in range(4):
+                queue.dma_start(out=dst[32 * quad:32 * quad + 4 * passes, :], in_=rows[:, 4 * quad:4 * quad + 4, :])
+
+        def load_vectors():
+            for row, vec in ((0, bx), (4, gain)):
+                nc.gpsimd.dma_start(
+                    out=vec_rows[row:row + 4].rearrange("t b (g q) -> t (b g) q", q=8),
+                    in_=vec.rearrange("(u t q) -> t u q", t=4, q=8),
+                )
+            nc.gpsimd.dma_start(out=vec_rows[8:12, 0, :], in_=sp.rearrange("(m p) -> m p", p=P))
+
+        nc.sync.dma_start(out=wy_w_raw[:], in_=wy_words[0].bitcast(I32))
+        load_scales(nc.sync, tab_s, tab_scales)
+        nc.sync.dma_start(out=list1[:], in_=offs)
+        load_words(tab_w[0], tab_words, 0)
+        nc.sync.dma_start(out=list2[:], in_=offs2)
+        load_wu(0, 0)
+        load_vectors()
+        make_identity(nc, ident[:])
+        load_scales(nc.scalar, tab2_s, tab2_scales)
+        load_words(tab2_w, tab2_words, 0)
+        load_scales(nc.sync, wy_s_raw, wy_scales)
+        load_wu(1, 0)
+        load_words(tab_w[1], tab_words, 1)
+        load_wu(0, 1)
+        load_wu(1, 1)
+        load_wp(0)
+        load_wp(1)
+
+        for b in range(2):
+            nc.tensor.transpose(vec_ps[:, b, :], vec_rows[:, b, :], ident[:])
+        nc.scalar.activation(out=neg_sp[:], in_=vec_ps[:, 0, 8:12], func=ACT.Copy, scale=-1.0)
+        nc.scalar.copy(out=bias[:], in_=vec_ps[:, :, 0:4])
+
+        def gather(dst, table, dtype, offsets, c):
+            cols = slice(c * CHUNK, (c + 1) * CHUNK)
+            picks = offsets[:, c * CHUNK // 16:(c + 1) * CHUNK // 16]
+            nc.vector.tensor_copy(out=dst[:, cols], in_=table[:].bitcast(dtype).indirect(picks))
+
+        def copy_on(engine, dst, src):
+            if engine == "V":
+                nc.vector.tensor_copy(out=dst, in_=src)
+            elif engine == "G":
+                nc.gpsimd.tensor_scalar(out=dst, in0=src, scalar1=1.0, scalar2=0.0, op0=ALU.mult, op1=ALU.add)
+            else:
+                nc.scalar.copy(out=dst, in_=src)
+
+        def cast_wu(a, b, engines):
+            src = wu_raw[a, b][:].rearrange("p j (g t h i) -> p t g h j i", t=4, h=2, i=4)
+            dst = wu_bf[a, b][:].rearrange("p (t g h i) j -> p t g h j i", t=4, h=2, i=4)
+            for t in range(4):
+                copy_on(engines[t], dst[:, t], src[:, t])
+
+        def quantize(words, scales, values, cols):
+            nc.vector.quantize_mx(
+                out=words[:, cols].bitcast(FP8X4),
+                scales=scales[:, cols],
+                in_=values.rearrange("p c j -> p (c j)"),
+            )
+
+        def quant_wu(a, b, pieces):
+            width = PASS // pieces
+            for i in range(pieces):
+                cols = slice(i * width, (i + 1) * width)
+                quantize(wu_w[a, b], wu_s[a, b], wu_bf[a, b][:, cols, :], cols)
+
+        def cast_wp(b, engines):
+            src = wp_raw[b][:].rearrange("p t (c i) -> p c t i", i=4)
+            dst = wp_bf[b][:].rearrange("p (c i) t -> p c t i", i=4)
+            for m in range(4):
+                part = slice(m * 32, (m + 1) * 32)
+                copy_on(engines[m], dst[:, part], src[:, part])
+
+        def quant_wp(b):
+            quantize(wp_w[b], wp_s[b], wp_bf[b][:], slice(0, N))
+
+        def state_sums(b, c, pieces):
+            cols = slice(c * CHUNK, (c + 1) * CHUNK)
+            zs = [psum.tile([P, CHUNK], F32, name="acc", tag="acc") for t in range(4)]
+
+            def wu_pass(a, t, start, stop):
+                m = slice(t * P, (t + 1) * P)
+                nc.tensor.matmul_mx(
+                    out=zs[t][:], lhsT=wu_w[a, b][:, m].bitcast(FP8X4), lhsT_scale=wu_s[a, b][:, m],
+                    rhs=v_w[a][:, cols].bitcast(FP8X4), rhs_scale=v_s[4 * a:P, cols], start=start, stop=stop)
+
+            def wy_pass(t, start):
+                col0 = b * PASS + t * P
+                nc.tensor.matmul_mx(
+                    out=zs[t][:],
+                    lhsT=wy_w[:].bitcast(U8)[:, 2 * col0:2 * (col0 + P)].bitcast(FP4X4),
+                    lhsT_scale=wy_s[:].bitcast(U8)[:, col0:col0 + P],
+                    rhs=v2_w[:, cols].bitcast(FP8X4), rhs_scale=v2_s[:, cols], start=start, stop=False)
+
+            for t in range(4):
+                if b == 0:
+                    wu_pass(0, t, True, False)
+                else:
+                    wy_pass(t, True)
+            for t in range(4):
+                if b == 0:
+                    wy_pass(t, False)
+                else:
+                    wu_pass(0, t, False, False)
+            for t in range(4):
+                wu_pass(1, t, False, True)
+            width = CHUNK // pieces
+            for i in range(pieces):
+                part = slice(i * width, (i + 1) * width)
+                for t in range(4):
+                    nc.scalar.activation(
+                        out=th[b, c][:, t, part], in_=zs[t][:, part], func=ACT.Tanh, bias=bias[:, b, t:t + 1])
+
+        def state(b, c, j0, width):
+            nc.vector.tensor_tensor(
+                out=xb[b, c][:, j0:j0 + width, :].rearrange("p (c i) t -> p c t i", i=4),
+                in0=th[b, c][:, :, j0:j0 + width].rearrange("p t (c i) -> p c t i", i=4),
+                in1=vec_ps[:, b, 4:8].unsqueeze(1).unsqueeze(3).to_broadcast([P, width // 4, 4, 4]),
+                op=ALU.mult,
+            )
+
+        def quant_x(b, c, j0, width):
+            quantize(x_w[b], x_s[b], xb[b, c][:, j0:j0 + width, :], slice(c * CHUNK + j0, c * CHUNK + j0 + width))
+
+        def predict(c, j0, width, engines):
+            cols = slice(c * CHUNK + j0, c * CHUNK + j0 + width)
+            ys = [psum.tile([P, width], F32, name="acc", tag="acc") for m in range(4)]
+            for b in range(2):
+                for m in range(4):
+                    n_cols = slice(m * P, (m + 1) * P)
+                    nc.tensor.matmul_mx(
+                        out=ys[m][:], lhsT=wp_w[b][:, n_cols].bitcast(FP8X4), lhsT_scale=wp_s[b][:, n_cols],
+                        rhs=x_w[b][:, cols].bitcast(FP8X4), rhs_scale=x_s[b][:, cols],
+                        start=(b == 0), stop=(b == 1))
+            rows = out.rearrange("(m p) j -> p m j", p=P)
+            for m in range(4):
+                if engines[m] == "V":
+                    nc.vector.tensor_scalar(
+                        out=res[:, m, cols], in0=ys[m][:], scalar1=neg_sp[:, m:m + 1], scalar2=None, op0=ALU.add)
+                else:
+                    nc.scalar.activation(out=res[:, m, cols], in_=ys[m][:], func=ACT.Identity, bias=neg_sp[:, m:m + 1])
+                if m % 2 == 1:
+                    nc.sync.dma_start(out=rows[:, m - 1:m + 1, cols], in_=res[:, m - 1:m + 1, cols])
+
+        def permute_wy():
+            nc.vector.tensor_copy(
+                out=wy_w[:].rearrange("p (b t g w) -> p b t g w", b=2, t=4, w=4),
+                in_=wy_w_raw[:].rearrange("p (b g t w) -> p b t g w", b=2, t=4, w=4))
+            nc.vector.tensor_copy(
+                out=wy_s[:].rearrange("p (b t g w) -> p b t g w", b=2, t=4, w=2),
+                in_=wy_s_raw[:].rearrange("p (b g t w) -> p b t g w", b=2, t=4, w=2))
+
+        gather(v_s, tab_s, U8, list1, 0)
+        gather(v_w[0], tab_w[0], U32, list1, 0)
+        gather(v2_s, tab2_s, U8, list2, 0)
+        gather(v2_w, tab2_w, U32, list2, 0)
+        gather(v_w[1], tab_w[1], U32, list1, 0)
+        permute_wy()
+        cast_wu(0, 0, "SSSS")
+        cast_wu(1, 0, "SSSS")
+        quant_wu(0, 0, 2)
+        quant_wu(1, 0, 2)
+        state_sums(0, 0, 2)
+        gather(v_s, tab_s, U8, list1, 1)
+        gather(v_w[0], tab_w[0], U32, list1, 1)
+        gather(v2_s, tab2_s, U8, list2, 1)
+        gather(v2_w, tab2_w, U32, list2, 1)
+        gather(v_w[1], tab_w[1], U32, list1, 1)
+        cast_wu(0, 1, "VVSS")
+        cast_wu(1, 1, "VVSS")
+        quant_wu(0, 1, 1)
+        quant_wu(1, 1, 2)
+        state_sums(0, 1, 1)
+        cast_wp(0, "VVSS")
+        cast_wp(1, "VVVS")
+        quant_wp(0)
+        quant_wp(1)
+        state_sums(1, 0, 2)
+        state_sums(1, 1, 2)
+        state(0, 0, 0, 256)
+        state(0, 0, 256, 256)
+        quant_x(0, 0, 0, 512)
+        state(0, 1, 0, 512)
+        state(1, 0, 0, 256)
+        state(1, 0, 256, 256)
+        quant_x(1, 0, 0, 256)
+        quant_x(1, 0, 256, 256)
+        predict(0, 0, 256, "SSSS")
+        predict(0, 256, 256, "SSSS")
+        state(1, 1, 0, 256)
+        quant_x(0, 1, 0, 512)
+        quant_x(1, 1, 0, 256)
+        predict(1, 0, 256, "SSSS")
+        state(1, 1, 256, 256)
+        quant_x(1, 1, 256, 256)
+        predict(1, 256, 256, "SVSV")

@@ -72,7 +72,7 @@ def tile_list_predictive_control_error_kernel(
         nc.gpsimd.memset(tab_s[:], 0)
         nc.vector.memset(tab2_s[:], 0)
         nc.gpsimd.memset(vec_rows[:], 0.0)
-        nc.gpsimd.memset(wy_s_raw[:], 0)
+        nc.vector.memset(wy_s_raw[:], 0)
 
         def load_words(dst, words, a):
             nc.sync.dma_start(out=dst[:], in_=words[a].rearrange("p t i -> p (t i)").bitcast(I32))
@@ -86,11 +86,15 @@ def tile_list_predictive_control_error_kernel(
             for t in range(4):
                 nc.sync.dma_start(out=wp_raw[b][:, t, :], in_=rows[t])
 
-        def load_scales(queue, dst, scales):
-            passes = scales.shape[0]
+        def load_packed_scales(queue, dst, scales):
             rows = scales.bitcast(I32)
-            for quad in range(4):
-                queue.dma_start(out=dst[32 * quad:32 * quad + 4 * passes, :], in_=rows[:, 4 * quad:4 * quad + 4, :])
+            for quad in (0, 2, 1, 3):
+                queue.dma_start(out=dst[32 * quad:32 * quad + 8, :], in_=rows[:, 4 * quad:4 * quad + 4, :])
+
+        def load_scales(queue, dst, scales):
+            rows = scales[0].bitcast(I32).rearrange("(quad r) w -> r quad w", r=4)
+            for r in range(4):
+                queue.dma_start(out=dst[r:P:32, :], in_=rows[r])
 
         def load_vectors():
             for row, vec in ((0, bx), (4, gain)):
@@ -101,7 +105,7 @@ def tile_list_predictive_control_error_kernel(
             nc.gpsimd.dma_start(out=vec_rows[8:12, 0, :], in_=sp.rearrange("(m p) -> m p", p=P))
 
         nc.sync.dma_start(out=wy_w_raw[:], in_=wy_words[0].bitcast(I32))
-        load_scales(nc.sync, tab_s, tab_scales)
+        load_packed_scales(nc.sync, tab_s, tab_scales)
         nc.sync.dma_start(out=list1[:], in_=offs)
         load_words(tab_w[0], tab_words, 0)
         nc.sync.dma_start(out=list2[:], in_=offs2)

@@ -66,6 +66,7 @@ def tile_list_predictive_control_error_kernel(
         vec_rows = held("vec_rows", [P, 2, P], F32)
         ident = held("ident", [P, P], F32)
         bias = held("bias", [P, 2, 4], F32)
+        sp_col = held("sp_col", [P, 4], F32)
         neg_sp = held("neg_sp", [P, 4], F32)
         vec_ps = psum_vec.tile([P, 2, P], F32, name="vec_ps")
 
@@ -98,22 +99,21 @@ def tile_list_predictive_control_error_kernel(
 
         def load_vectors():
             for row, vec in ((0, bx), (4, gain)):
-                nc.gpsimd.dma_start(
+                nc.scalar.dma_start(
                     out=vec_rows[row:row + 4].rearrange("t b (g q) -> t (b g) q", q=8),
                     in_=vec.rearrange("(u t q) -> t u q", t=4, q=8),
                 )
-            nc.gpsimd.dma_start(out=vec_rows[8:12, 0, :], in_=sp.rearrange("(m p) -> m p", p=P))
 
         nc.sync.dma_start(out=wy_w_raw[:], in_=wy_words[0].bitcast(I32))
         load_packed_scales(nc.sync, tab_s, tab_scales)
         nc.sync.dma_start(out=list1[:], in_=offs)
         load_words(tab_w[0], tab_words, 0)
-        nc.sync.dma_start(out=list2[:], in_=offs2)
         load_wu(0, 0)
+        load_scales(nc.scalar, tab2_s, tab2_scales)
+        nc.sync.dma_start(out=list2[:], in_=offs2)
+        load_words(tab2_w, tab2_words, 0)
         load_vectors()
         make_identity(nc, ident[:])
-        load_scales(nc.scalar, tab2_s, tab2_scales)
-        load_words(tab2_w, tab2_words, 0)
         load_scales(nc.sync, wy_s_raw, wy_scales)
         load_wu(1, 0)
         load_words(tab_w[1], tab_words, 1)
@@ -121,11 +121,13 @@ def tile_list_predictive_control_error_kernel(
         load_wu(1, 1)
         load_wp(0)
         load_wp(1)
+        with nc.allow_non_contiguous_dma(reason="one set point a partition and output tile"):
+            nc.sync.dma_start(out=sp_col[:], in_=sp.rearrange("(m p) -> p m", p=P))
 
         for b in range(2):
             nc.tensor.transpose(vec_ps[:, b, :], vec_rows[:, b, :], ident[:])
-        nc.scalar.activation(out=neg_sp[:], in_=vec_ps[:, 0, 8:12], func=ACT.Copy, scale=-1.0)
-        nc.scalar.copy(out=bias[:], in_=vec_ps[:, :, 0:4])
+        nc.scalar.activation(out=bias[:], in_=vec_ps[:, :, 0:4], func=ACT.Copy)
+        nc.scalar.activation(out=neg_sp[:], in_=sp_col[:], func=ACT.Copy, scale=-1.0)
 
         def gather(dst, table, dtype, offsets, c):
             cols = slice(c * CHUNK, (c + 1) * CHUNK)
@@ -141,8 +143,8 @@ def tile_list_predictive_control_error_kernel(
                 nc.scalar.copy(out=dst, in_=src)
 
         def cast_wu(a, b, engines):
-            src = wu_raw[a, b][:].rearrange("p j (g t h i) -> p t g h j i", t=4, h=2, i=4)
-            dst = wu_bf[a, b][:].rearrange("p (t g h i) j -> p t g h j i", t=4, h=2, i=4)
+            src = wu_raw[a, b][:].rearrange("p j (g t h i) -> p t g h j i", t=4, h=4, i=2)
+            dst = wu_bf[a, b][:].rearrange("p (t g h i) j -> p t g h j i", t=4, h=4, i=2)
             for t in range(4):
                 copy_on(engines[t], dst[:, t], src[:, t])
 
@@ -160,10 +162,10 @@ def tile_list_predictive_control_error_kernel(
                 quantize(wu_w[a, b], wu_s[a, b], wu_bf[a, b][:, cols, :], cols)
 
         def cast_wp(b, engines):
-            src = wp_raw[b][:].rearrange("p t (c i) -> p c t i", i=4)
-            dst = wp_bf[b][:].rearrange("p (c i) t -> p c t i", i=4)
+            src = wp_raw[b][:].rearrange("p t (c i) -> p c t i", i=2)
+            dst = wp_bf[b][:].rearrange("p (c i) t -> p c t i", i=2)
             for m in range(4):
-                part = slice(m * 32, (m + 1) * 32)
+                part = slice(m * 64, (m + 1) * 64)
                 copy_on(engines[m], dst[:, part], src[:, part])
 
         def quant_wp(b):
@@ -208,9 +210,9 @@ def tile_list_predictive_control_error_kernel(
 
         def state(b, c, j0, width):
             nc.vector.tensor_tensor(
-                out=xb[b, c][:, j0:j0 + width, :].rearrange("p (c i) t -> p c t i", i=4),
-                in0=th[b, c][:, :, j0:j0 + width].rearrange("p t (c i) -> p c t i", i=4),
-                in1=vec_ps[:, b, 4:8].unsqueeze(1).unsqueeze(3).to_broadcast([P, width // 4, 4, 4]),
+                out=xb[b, c][:, j0:j0 + width, :].rearrange("p (c i) t -> p c t i", i=2),
+                in0=th[b, c][:, :, j0:j0 + width].rearrange("p t (c i) -> p c t i", i=2),
+                in1=vec_ps[:, b, 4:8].unsqueeze(1).unsqueeze(3).to_broadcast([P, width // 2, 4, 2]),
                 op=ALU.mult,
             )
 

from contextlib import ExitStack

import concourse.mybir as mybir
from concourse.masks import make_identity

K, K2, H, N, T, S = 1024, 512, 1024, 512, 2048, 1024
FLOPS = 2 * S * (K * H + K2 * H + H * N)

F32 = mybir.dt.float32
BF16 = mybir.dt.bfloat16
I32 = mybir.dt.int32
U32 = mybir.dt.uint32
U16 = mybir.dt.uint16
U8 = mybir.dt.uint8
FP8X4 = mybir.dt.float8_e4m3fn_x4
FP4X4 = mybir.dt.float4_e2m1fn_x4
ACT = mybir.ActivationFunctionType
ALU = mybir.AluOpType

P = 128
PASS = 512
CHUNK = 512
AL = 64


def tile_list_predictive_control_error_kernel(
    tc, tab_words, tab_scales, offs, tab2_words, tab2_scales, offs2,
    wu, wy_words, wy_scales, bx, gain, wp, sp, out,
):
    nc = tc.nc
    with ExitStack() as ctx:
        keep = ctx.enter_context(tc.tile_pool(name="keep", bufs=1))
        psum_vec = ctx.enter_context(tc.psum_pool(name="psum_vec", bufs=1))
        psum = ctx.enter_context(tc.psum_pool(name="psum", bufs=7))

        def held(name, shape, dtype):
            return keep.tile(shape, dtype, name=name, align_bytes=AL)

        list1 = held("list1", [P, S // 16], U16)
        list2 = held("list2", [P, S // 16], U16)
        tab_w = [held("tab_w%d" % a, [P, T], I32) for a in range(2)]
        tab2_w = held("tab2_w", [P, T], I32)
        tab_s = held("tab_s", [P, T // 4], I32)
        tab2_s = held("tab2_s", [P, T // 4], I32)
        wy_w_raw = held("wy_w_raw", [P, H // 2], I32)
        wy_s_raw = held("wy_s_raw", [P, H // 4], I32)
        wy_w = held("wy_w", [P, H // 2], I32)
        wy_s = held("wy_s", [P, H // 4], I32)
        v_w = [held("v_w%d" % a, [P, S], U32) for a in range(2)]
        v_s = held("v_s", [P, S], U8)
        v2_w = held("v2_w", [P, S], U32)
        v2_s = held("v2_s", [P, S], U8)
        wu_raw = {(a, b): held("wu_raw%d%d" % (a, b), [P, 4, PASS], F32) for a in range(2) for b in range(2)}
        wu_bf = {(a, b): held("wu_bf%d%d" % (a, b), [P, PASS, 4], BF16) for a in range(2) for b in range(2)}
        wu_w = {(a, b): held("wu_w%d%d" % (a, b), [P, PASS], U32) for a in range(2) for b in range(2)}
        wu_s = {(a, b): held("wu_s%d%d" % (a, b), [P, PASS], U8) for a in range(2) for b in range(2)}
        wp_raw = [held("wp_raw%d" % b, [P, 4, N], F32) for b in range(2)]
        wp_bf = [held("wp_bf%d" % b, [P, N, 4], BF16) for b in range(2)]
        wp_w = [held("wp_w%d" % b, [P, N], U32) for b in range(2)]
        wp_s = [held("wp_s%d" % b, [P, N], U8) for b in range(2)]
        x_w = [held("x_w%d" % b, [P, S], U32) for b in range(2)]
        x_s = [held("x_s%d" % b, [P, S], U8) for b in range(2)]
        th = {(b, c): held("th%d%d" % (b, c), [P, 4, CHUNK], F32) for b in range(2) for c in range(2)}
        xb = {(b, c): held("xb%d%d" % (b, c), [P, CHUNK, 4], BF16) for b in range(2) for c in range(2)}
        res = held("res", [P, 4, S], F32)
        vec_rows = held("vec_rows", [P, 2, P], F32)
        ident = held("ident", [P, P], F32)
        bias = held("bias", [P, 2, 4], F32)
        sp_col = held("sp_col", [P, 4], F32)
        neg_sp = held("neg_sp", [P, 4], F32)
        vec_ps = psum_vec.tile([P, 2, P], F32, name="vec_ps")

        nc.gpsimd.memset(tab_s[:], 0)
        nc.vector.memset(tab2_s[:], 0)
        nc.gpsimd.memset(vec_rows[:], 0.0)
        nc.vector.memset(wy_s_raw[:], 0)

        def load_words(dst, words, a):
            nc.sync.dma_start(out=dst[:], in_=words[a].rearrange("p t i -> p (t i)").bitcast(I32))

        def load_wu(a, b):
            rows = wu[a * PASS:(a + 1) * PASS, b * PASS:(b + 1) * PASS]
            nc.sync.dma_start(out=wu_raw[a, b][:], in_=rows.rearrange("(p j) c -> p j c", j=4))

        def load_wp(b):
            rows = wp[b * PASS:(b + 1) * PASS, :].rearrange("(g t q) n -> t g q n", t=4, q=8)
            for t in range(4):
                nc.sync.dma_start(out=wp_raw[b][:, t, :], in_=rows[t])

        def load_packed_scales(queue, dst, scales):
            rows = scales.bitcast(I32)
            for quad in (0, 2, 1, 3):
                queue.dma_start(out=dst[32 * quad:32 * quad + 8, :], in_=rows[:, 4 * quad:4 * quad + 4, :])

        def load_scales(queue, dst, scales):
            rows = scales[0].bitcast(I32).rearrange("(quad r) w -> r quad w", r=4)
            for r in range(4):
                queue.dma_start(out=dst[r:P:32, :], in_=rows[r])

        def load_vectors():
            for row, vec in ((0, bx), (4, gain)):
                nc.scalar.dma_start(
                    out=vec_rows[row:row + 4].rearrange("t b (g q) -> t (b g) q", q=8),
                    in_=vec.rearrange("(u t q) -> t u q", t=4, q=8),
                )

        nc.sync.dma_start(out=wy_w_raw[:], in_=wy_words[0].bitcast(I32))
        load_packed_scales(nc.sync, tab_s, tab_scales)
        nc.sync.dma_start(out=list1[:], in_=offs)
        load_words(tab_w[0], tab_words, 0)
        load_wu(0, 0)
        load_scales(nc.scalar, tab2_s, tab2_scales)
        nc.sync.dma_start(out=list2[:], in_=offs2)
        load_words(tab2_w, tab2_words, 0)
        load_vectors()
        make_identity(nc, ident[:])
        load_scales(nc.sync, wy_s_raw, wy_scales)
        load_wu(1, 0)
        load_words(tab_w[1], tab_words, 1)
        load_wu(0, 1)
        load_wu(1, 1)
        load_wp(0)
        load_wp(1)
        with nc.allow_non_contiguous_dma(reason="one set point a partition and output tile"):
            nc.sync.dma_start(out=sp_col[:], in_=sp.rearrange("(m p) -> p m", p=P))

        for b in range(2):
            nc.tensor.transpose(vec_ps[:, b, :], vec_rows[:, b, :], ident[:])
        nc.scalar.activation(out=bias[:], in_=vec_ps[:, :, 0:4], func=ACT.Copy)
        nc.scalar.activation(out=neg_sp[:], in_=sp_col[:], func=ACT.Copy, scale=-1.0)

        def gather(dst, table, dtype, offsets, c):
            cols = slice(c * CHUNK, (c + 1) * CHUNK)
            picks = offsets[:, c * CHUNK // 16:(c + 1) * CHUNK // 16]
            nc.vector.tensor_copy(out=dst[:, cols], in_=table[:].bitcast(dtype).indirect(picks))

        def copy_on(engine, dst, src):
            if engine == "V":
                nc.vector.tensor_copy(out=dst, in_=src)
            elif engine == "G":
                nc.gpsimd.tensor_scalar(out=dst, in0=src, scalar1=1.0, scalar2=0.0, op0=ALU.mult, op1=ALU.add)
            else:
                nc.scalar.copy(out=dst, in_=src)

        def cast_wu(a, b, engines):
            src = wu_raw[a, b][:].rearrange("p j (g t h i) -> p t g h j i", t=4, h=4, i=2)
            dst = wu_bf[a, b][:].rearrange("p (t g h i) j -> p t g h j i", t=4, h=4, i=2)
            for t in range(4):
                copy_on(engines[t], dst[:, t], src[:, t])

        def quantize(words, scales, values, cols):
            nc.vector.quantize_mx(
                out=words[:, cols].bitcast(FP8X4),
                scales=scales[:, cols],
                in_=values.rearrange("p c j -> p (c j)"),
            )

        def quant_wu(a, b, pieces):
            width = PASS // pieces
            for i in range(pieces):
                cols = slice(i * width, (i + 1) * width)
                quantize(wu_w[a, b], wu_s[a, b], wu_bf[a, b][:, cols, :], cols)

        def cast_wp(b, engines):
            src = wp_raw[b][:].rearrange("p t (c i) -> p c t i", i=2)
            dst = wp_bf[b][:].rearrange("p (c i) t -> p c t i", i=2)
            for m in range(4):
                part = slice(m * 64, (m + 1) * 64)
                copy_on(engines[m], dst[:, part], src[:, part])

        def quant_wp(b):
            quantize(wp_w[b], wp_s[b], wp_bf[b][:], slice(0, N))

        def state_sums(b, c, pieces):
            cols = slice(c * CHUNK, (c + 1) * CHUNK)
            zs = [psum.tile([P, CHUNK], F32, name="acc", tag="acc") for t in range(4)]

            def wu_pass(a, t, start, stop):
                m = slice(t * P, (t + 1) * P)
                nc.tensor.matmul_mx(
                    out=zs[t][:], lhsT=wu_w[a, b][:, m].bitcast(FP8X4), lhsT_scale=wu_s[a, b][:, m],
                    rhs=v_w[a][:, cols].bitcast(FP8X4), rhs_scale=v_s[4 * a:P, cols], start=start, stop=stop)

            def wy_pass(t, start):
                col0 = b * PASS + t * P
                nc.tensor.matmul_mx(
                    out=zs[t][:],
                    lhsT=wy_w[:].bitcast(U8)[:, 2 * col0:2 * (col0 + P)].bitcast(FP4X4),
                    lhsT_scale=wy_s[:].bitcast(U8)[:, col0:col0 + P],
                    rhs=v2_w[:, cols].bitcast(FP8X4), rhs_scale=v2_s[:, cols], start=start, stop=False)

            for t in range(4):
                if b == 0:
                    wu_pass(0, t, True, False)
                else:
                    wy_pass(t, True)
            for t in range(4):
                if b == 0:
                    wy_pass(t, False)
                else:
                    wu_pass(0, t, False, False)
            for t in range(4):
                wu_pass(1, t, False, True)
            width = CHUNK // pieces
            for i in range(pieces):
                part = slice(i * width, (i + 1) * width)
                for t in range(4):
                    nc.scalar.activation(
                        out=th[b, c][:, t, part], in_=zs[t][:, part], func=ACT.Tanh, bias=bias[:, b, t:t + 1])

        def state(b, c, j0, width):
            nc.vector.tensor_tensor(
                out=xb[b, c][:, j0:j0 + width, :].rearrange("p (c i) t -> p c t i", i=2),
                in0=th[b, c][:, :, j0:j0 + width].rearrange("p t (c i) -> p c t i", i=2),
                in1=vec_ps[:, b, 4:8].unsqueeze(1).unsqueeze(3).to_broadcast([P, width // 2, 4, 2]),
                op=ALU.mult,
            )

        def quant_x(b, c, j0, width):
            quantize(x_w[b], x_s[b], xb[b, c][:, j0:j0 + width, :], slice(c * CHUNK + j0, c * CHUNK + j0 + width))

        def predict(c, j0, width, engines):
            cols = slice(c * CHUNK + j0, c * CHUNK + j0 + width)
            ys = [psum.tile([P, width], F32, name="acc", tag="acc") for m in range(4)]
            for b in range(2):
                for m in range(4):
                    n_cols = slice(m * P, (m + 1) * P)
                    nc.tensor.matmul_mx(
                        out=ys[m][:], lhsT=wp_w[b][:, n_cols].bitcast(FP8X4), lhsT_scale=wp_s[b][:, n_cols],
                        rhs=x_w[b][:, cols].bitcast(FP8X4), rhs_scale=x_s[b][:, cols],
                        start=(b == 0), stop=(b == 1))
            rows = out.rearrange("(m p) j -> p m j", p=P)
            for m in range(4):
                if engines[m] == "V":
                    nc.vector.tensor_scalar(
                        out=res[:, m, cols], in0=ys[m][:], scalar1=neg_sp[:, m:m + 1], scalar2=None, op0=ALU.add)
                else:
                    nc.scalar.activation(out=res[:, m, cols], in_=ys[m][:], func=ACT.Identity, bias=neg_sp[:, m:m + 1])
                if m % 2 == 1:
                    nc.sync.dma_start(out=rows[:, m - 1:m + 1, cols], in_=res[:, m - 1:m + 1, cols])

        def permute_wy():
            nc.vector.tensor_copy(
                out=wy_w[:].rearrange("p (b t g w) -> p b t g w", b=2, t=4, w=4),
                in_=wy_w_raw[:].rearrange("p (b g t w) -> p b t g w", b=2, t=4, w=4))
            nc.vector.tensor_copy(
                out=wy_s[:].rearrange("p (b t g w) -> p b t g w", b=2, t=4, w=2),
                in_=wy_s_raw[:].rearrange("p (b g t w) -> p b t g w", b=2, t=4, w=2))

        gather(v_s, tab_s, U8, list1, 0)
        gather(v_w[0], tab_w[0], U32, list1, 0)
        gather(v2_s, tab2_s, U8, list2, 0)
        gather(v2_w, tab2_w, U32, list2, 0)
        gather(v_w[1], tab_w[1], U32, list1, 0)
        permute_wy()
        cast_wu(0, 0, "SSSS")
        cast_wu(1, 0, "SSSS")
        quant_wu(0, 0, 2)
        quant_wu(1, 0, 2)
        state_sums(0, 0, 2)
        gather(v_s, tab_s, U8, list1, 1)
        gather(v_w[0], tab_w[0], U32, list1, 1)
        gather(v2_s, tab2_s, U8, list2, 1)
        gather(v2_w, tab2_w, U32, list2, 1)
        gather(v_w[1], tab_w[1], U32, list1, 1)
        cast_wu(0, 1, "VVSS")
        cast_wu(1, 1, "VVSS")
        quant_wu(0, 1, 1)
        quant_wu(1, 1, 2)
        state_sums(0, 1, 1)
        cast_wp(0, "VVSS")
        cast_wp(1, "VVVS")
        quant_wp(0)
        quant_wp(1)
        state_sums(1, 0, 2)
        state_sums(1, 1, 2)
        state(0, 0, 0, 256)
        state(0, 0, 256, 256)
        quant_x(0, 0, 0, 512)
        state(0, 1, 0, 512)
        state(1, 0, 0, 256)
        state(1, 0, 256, 256)
        quant_x(1, 0, 0, 256)
        quant_x(1, 0, 256, 256)
        predict(0, 0, 256, "SSSS")
        predict(0, 256, 256, "SSSS")
        state(1, 1, 0, 256)
        quant_x(0, 1, 0, 512)
        quant_x(1, 1, 0, 256)
        predict(1, 0, 256, "SSSS")
        state(1, 1, 256, 256)
        quant_x(1, 1, 256, 256)
        predict(1, 256, 256, "SVSV")
